import numpy as np
import ml_dtypes


def mxq(x, axis, fmt="e4m3"):
    dtype, down = {"e4m3": (ml_dtypes.float8_e4m3fn, 7), "e5m2": (ml_dtypes.float8_e5m2, 14)}[fmt]
    v = np.moveaxis(np.asarray(x, np.float32).astype(ml_dtypes.bfloat16).astype(np.float64), axis, -1)
    blocks = v.reshape(v.shape[:-1] + (-1, 32))
    amax = np.abs(blocks).max(-1, keepdims=True)
    byte = np.maximum(np.where(amax > 0, np.frexp(amax)[1] - 1 + 127, 0) - down, 1)
    scale = np.exp2(byte - 127.0)
    codes = (blocks / scale).astype(np.float32).astype(dtype).astype(np.float64)
    return np.moveaxis((codes * scale).reshape(v.shape), -1, axis)


WIDE = False


def mx_kscale(k):
    if not WIDE:
        return np.ones(k)
    levels = np.array([10, -10, 5, -5, 0])
    if k % 512:
        return np.exp2(np.random.permutation(np.resize(levels, k // 32))).repeat(32)
    a = np.empty((k // 512, 16))
    for p in range(k // 512):
        a[p, :8] = np.random.permutation(np.resize(levels, 8))
        for g in range(8):
            far = levels[np.abs(levels - a[p, g]) >= 10]
            a[p, g + 8] = far[np.random.randint(len(far))]
    return np.exp2(a.ravel()).repeat(32)


BF16 = ml_dtypes.bfloat16


def bf(x):
    return np.asarray(x, np.float32).astype(BF16)


def f64(x):
    return np.asarray(x).astype(np.float64)


E2M1 = np.array([0.0, 0.5, 1.0, 1.5, 2.0, 3.0, 4.0, 6.0, -0.0, -0.5, -1.0, -1.5, -2.0, -3.0, -4.0, -6.0])


def pack_weight(w, fmt):
    k, n = w.shape
    w = f64(bf(w)).reshape(k // 32, 32, n)
    amax = np.abs(w).max(1)
    if fmt == "e4m3":
        byte = np.frexp(amax)[1] - 1 + 127 - 7
    else:
        mant, ex = np.frexp(amax / 6.0)
        byte = np.where(mant > 0.5, ex, ex - 1) + 127
    byte = np.clip(np.where(amax > 0, byte, 1), 1, 254)
    scaled = (w * np.exp2(127.0 - byte)[:, None, :]).reshape(k, n).astype(np.float32)
    by_word = np.ascontiguousarray(scaled.reshape(k // 512, 128, 4, n).transpose(0, 1, 3, 2))
    if fmt == "e4m3":
        words = by_word.astype(ml_dtypes.float8_e4m3fn).view(np.uint8)
    else:
        c = by_word.astype(ml_dtypes.float4_e2m1fn).view(np.uint8) & 0xF
        words = c[..., 0::2] | (c[..., 1::2] << 4)
    return np.ascontiguousarray(words), np.ascontiguousarray(byte.astype(np.uint8).reshape(k // 512, 16, n))


def unpack_weight(words, scales, fmt):
    g, p, n, _ = words.shape
    if fmt == "e4m3":
        vals = np.ascontiguousarray(words).view(ml_dtypes.float8_e4m3fn).astype(np.float64)
    else:
        nib = np.empty((g, p, n, 4), np.uint8)
        nib[..., 0::2] = words & 0xF
        nib[..., 1::2] = words >> 4
        vals = E2M1[nib]
    vals = vals * np.repeat(np.exp2(scales.astype(np.float64) - 127.0), 8, axis=1)[..., None]
    return vals.transpose(0, 1, 3, 2).reshape(g * 512, n)

def planes(Y):
    n, m = Y.shape
    b = f64(bf(Y)).reshape(n // 32, 32, m)
    amax = np.abs(b).max(1)
    byte = np.clip(np.where(amax > 0, np.frexp(amax)[1] - 1 + 127 - 7, 1), 1, 254)
    codes = (b * np.exp2(127.0 - byte)[:, None, :]).reshape(n, m).astype(np.float32).astype(ml_dtypes.float8_e4m3fn).view(np.uint8)
    words = codes.reshape(n // 512, 128, 4, m).transpose(0, 1, 3, 2)
    return np.ascontiguousarray(words), np.ascontiguousarray(byte.astype(np.uint8).reshape(n // 512, 16, m))


P, K, W, N = 1024, 512, 1024, 512


def sigmoid(a):
    return 1.0 / (1.0 + np.exp(-a))


def setup_inputs():
    sv, sr, sl = mx_kscale(K), mx_kscale(K), mx_kscale(K)
    t = mx_kscale(W)
    c = 1.0 / np.sqrt(K)
    v = bf(np.random.standard_normal((P, K)) * sv)
    psi_words, psi_scales = pack_weight(np.random.standard_normal((K, W)) * c / sv[:, None], "e4m3")
    r = bf(np.random.standard_normal((P, K)) * 2.0 * sr)
    phi_words, phi_scales = pack_weight(np.random.standard_normal((K, W)) * c / sr[:, None] * t, "e4m3")
    q = bf(np.random.uniform(0.5, 1.5, W))
    l = bf(np.random.standard_normal((N, K)) * sl)
    theta_words, theta_scales = pack_weight(np.random.standard_normal((K, W)) * c / sl[:, None] / t, "e4m3")
    return {
        "v": v,
        "psi_words": psi_words,
        "psi_scales": psi_scales,
        "r": r,
        "phi_words": phi_words,
        "phi_scales": phi_scales,
        "q": q,
        "l": l,
        "theta_words": theta_words,
        "theta_scales": theta_scales,
    }


def core(v, psi_words, psi_scales, r, phi_words, phi_scales, q, l, theta_words, theta_scales):
    num_dirs = psi_words.shape[2]
    vis = sigmoid(mxq(f64(v), 1, "e4m3") @ unpack_weight(psi_words, psi_scales, "e4m3"))
    refl = mxq(f64(r), 1, "e4m3") @ unpack_weight(phi_words, phi_scales, "e4m3")
    tr = vis * refl * f64(q)[None, :]
    rad = mxq(f64(l), 1, "e4m3") @ unpack_weight(theta_words, theta_scales, "e4m3")
    coef = 4.0 * np.pi / num_dirs
    return coef * (mxq(tr, 1, "e4m3") @ mxq(rad, 1, "e4m3").T)


def reference(v, psi_words, psi_scales, r, phi_words, phi_scales, q, l, theta_words, theta_scales):
    R_out = core(v, psi_words, psi_scales, r, phi_words, phi_scales, q, l, theta_words, theta_scales)
    words, scales = planes(R_out)
    return R_out, words, scales

@@ -1,0 +1,346 @@
+import math
+
+import concourse.mybir as mybir
+from concourse.masks import make_identity
+
+F32 = mybir.dt.float32
+BF16 = mybir.dt.bfloat16
+I32 = mybir.dt.int32
+U32 = mybir.dt.uint32
+U8 = mybir.dt.uint8
+FP8X4 = mybir.dt.float8_e4m3fn_x4
+COPY = mybir.ActivationFunctionType.Copy
+SIGMOID = mybir.ActivationFunctionType.Sigmoid
+MULT = mybir.AluOpType.mult
+
+P, K, W, N = 1024, 512, 1024, 512
+FLOPS = 2 * (2 * P * K * W + N * K * W + P * W * N)
+COEF = 4.0 * math.pi / W
+
+
+def tile_tripleproductvisibilityreflectancereligh_x2_kernel(
+    tc, v, psi_words, psi_scales, r, phi_words, phi_scales, q, l, theta_words, theta_scales, out_0, out_1, out_2
+):
+    nc = tc.nc
+    with (
+        tc.tile_pool(name="keep", bufs=1) as keep,
+        tc.tile_pool(name="work", bufs=2) as work,
+        tc.psum_pool(name="psum", bufs=2) as psum,
+        tc.manual_schedule(),
+    ):
+        x_raw = {}
+
+        def load_rows(name, src, c, order="(p t) k -> p t k"):
+            for h in range(2):
+                t = keep.tile([128, 2, K], BF16, name=f"{name}_raw{h}", align_bytes=64)
+                nc.sync.dma_start(
+                    out=t[:], in_=src[512 * c : 512 * c + 512, :].rearrange(order, t=4)[:, 2 * h : 2 * h + 2, :]
+                )
+                x_raw[name, h] = t
+
+        def load_scales(dst, k, src):
+            for s in range(4):
+                nc.sync.dma_start(
+                    out=dst[32 * s + k : 32 * s + k + 4, :].bitcast(I32), in_=src[0, 4 * s : 4 * s + 4, :].bitcast(I32)
+                )
+
+        w_raw = {}
+
+        def load_words(name, src):
+            t = keep.tile([128, W], U32, name=f"{name}_raw", align_bytes=64)
+            nc.sync.dma_start(out=t[:].bitcast(I32), in_=src[0].rearrange("p n t -> p (n t)").bitcast(I32))
+            w_raw[name] = t
+
+        psi_s_raw = keep.tile([128, W], U8, name="psi_s_raw", align_bytes=64)
+        pt_s_raw = keep.tile([128, W], U8, name="pt_s_raw", align_bytes=64)
+        nc.vector.memset(psi_s_raw[:].bitcast(I32), 0)
+        nc.vector.memset(pt_s_raw[:].bitcast(I32), 0)
+        ident = keep.tile([128, 128], F32, name="ident", align_bytes=64)
+        make_identity(nc, ident[:])
+        warm = keep.tile([128, 1], F32, name="warm")
+        nc.vector.memset(warm[:], 0.0)
+        warmed = keep.tile([128, 1], F32, name="warmed")
+        nc.scalar.activation(out=warmed[:], in_=warm[:], func=SIGMOID)
+        q_sb = keep.tile([128, 2, 4], BF16, name="q_sb")
+        nc.gpsimd.dma_start(out=q_sb[:], in_=q.rearrange("(g p t) -> p g t", g=2, t=4))
+
+        load_rows("v0", v, 0)
+        load_scales(psi_s_raw, 0, psi_scales)
+        load_words("psi", psi_words)
+        load_rows("r0", r, 0)
+        load_scales(pt_s_raw, 0, phi_scales)
+        load_scales(pt_s_raw, 4, theta_scales)
+        load_words("phi", phi_words)
+        load_rows("l", l, 0, "(t p) k -> p t k")
+        load_words("the", theta_words)
+        load_rows("v1", v, 1)
+        load_rows("r1", r, 1)
+
+        xt, xq, xs = {}, {}, {}
+
+        def bank(tag):
+            t = psum.tile([128, 512], F32, name=tag)
+            return t
+
+        def turn(name, h, eng):
+            words = x_raw[name, h][:].rearrange("p t k -> p (t k)").bitcast(F32)
+            b = bank("tp")
+            for a in range(2):
+                for u in range(2):
+                    nc.tensor.transpose(
+                        b[:, 256 * a + 128 * u : 256 * a + 128 * u + 128], words[:, 256 * a + u : 256 * (a + 1) : 2], ident[:]
+                    )
+            if h == 0 or name not in xt:
+                if name not in xt:
+                    xt[name] = work.tile([128, 512, 4], BF16, name="xt", align_bytes=64)
+            dst = (
+                xt[name][:, 256 * h : 256 * h + 256, :]
+                .rearrange("p n t -> p (n t)")
+                .bitcast(F32)
+                .rearrange("p (a r u) -> p a r u", a=2, u=2)
+            )
+            src = b[:].rearrange("p (a u r) -> p a r u", a=2, u=2)
+            if eng == "S":
+                nc.scalar.copy(out=dst, in_=src)
+            else:
+                nc.vector.tensor_copy(out=dst, in_=src)
+
+        def quant(name):
+            xq[name] = keep.tile([128, 512], U32, name=f"{name}_q", align_bytes=64)
+            xs[name] = keep.tile([128, 512], U8, name=f"{name}_s", align_bytes=64)
+            nc.vector.quantize_mx(
+                out=xq[name][:].bitcast(FP8X4), scales=xs[name][:], in_=xt[name][:].rearrange("p n t -> p (n t)")
+            )
+
+        wp = {n: keep.tile([128, W], U32, name=f"{n}_p", align_bytes=64) for n in ("psi", "phi", "the")}
+        psi_s = keep.tile([128, W], U8, name="psi_s", align_bytes=64)
+        pt_s = keep.tile([128, W], U8, name="pt_s", align_bytes=64)
+
+        def scale_plane(name):
+            return {"psi": (psi_s, 0), "phi": (pt_s, 0), "the": (pt_s, 4)}[name]
+
+        def order_scales(dst, src):
+            nc.vector.tensor_copy(
+                out=dst[:].rearrange("p (g j m) -> p g m j", g=2, j=4), in_=src[:].rearrange("p (g m j) -> p g m j", g=2, j=4)
+            )
+
+        def order_words(name, g):
+            cols = slice(512 * g, 512 * g + 512)
+            nc.vector.tensor_copy(
+                out=wp[name][:, cols].bitcast(I32).rearrange("p (j m) -> p m j", j=4),
+                in_=w_raw[name][:, cols].bitcast(I32).rearrange("p (m j) -> p m j", j=4),
+            )
+
+        def product(dst, name, g, j, x, cols):
+            c0 = 512 * g + 128 * j
+            plane, k = scale_plane(name)
+            nc.tensor.matmul_mx(
+                out=dst,
+                lhsT=wp[name][:, c0 : c0 + 128].bitcast(FP8X4),
+                lhsT_scale=plane[k:128, c0 : c0 + 128],
+                rhs=xq[x][:, cols].bitcast(FP8X4),
+                rhs_scale=xs[x][:, cols],
+                start=True,
+                stop=True,
+            )
+
+        vis, tr, ti, tq, ts = {}, {}, {}, {}, {}
+        ALL = slice(0, 512)
+
+        def visible(c, g, h):
+            for j in (2 * h, 2 * h + 1):
+                b = bank("vis")
+                product(b[:], "psi", g, j, f"v{c}", ALL)
+                vis[c, g, j] = work.tile([128, 512], F32, name="vs", bufs=8, align_bytes=64)
+                nc.scalar.activation(out=vis[c, g, j][:], in_=b[:], func=SIGMOID)
+
+        def reflect(c, g, h):
+            if (c, g) not in tr:
+                tr[c, g] = work.tile([128, 4, 512], BF16, name="tr", bufs=3, align_bytes=64)
+            for j in (2 * h, 2 * h + 1):
+                b = bank("ref")
+                product(b[:], "phi", g, j, f"r{c}", ALL)
+                nc.vector.scalar_tensor_tensor(
+                    out=tr[c, g][:, j, :], in0=b[:], scalar=q_sb[:, g, j : j + 1], in1=vis[c, g, j][:], op0=MULT, op1=MULT
+                )
+
+        def interleave(c, g, cols, eng):
+            if (c, g) not in ti:
+                ti[c, g] = work.tile([128, 512, 4], BF16, name="ti", bufs=3, align_bytes=64)
+            dst = ti[c, g][:, cols, :]
+            src = tr[c, g][:, :, cols].rearrange("p j n -> p n j")
+            if eng == "S":
+                nc.scalar.copy(out=dst, in_=src)
+            else:
+                nc.vector.tensor_copy(out=dst, in_=src)
+
+        def quant_tr(c, g, cols):
+            if (c, g) not in tq:
+                tq[c, g] = keep.tile([128, 512], U32, name=f"tq{c}{g}", align_bytes=64)
+                ts[c, g] = keep.tile([128, 512], U8, name=f"ts{c}{g}", align_bytes=64)
+            nc.vector.quantize_mx(
+                out=tq[c, g][:, cols].bitcast(FP8X4),
+                scales=ts[c, g][:, cols],
+                in_=ti[c, g][:, cols, :].rearrange("p n j -> p (n j)"),
+            )
+
+        rt = {g: keep.tile([128, N, 4], BF16, name=f"rt{g}", align_bytes=64) for g in range(2)}
+        rq = {g: keep.tile([128, N], U32, name=f"rq{g}", align_bytes=64) for g in range(2)}
+        rs = {g: keep.tile([128, N], U8, name=f"rs{g}", align_bytes=64) for g in range(2)}
+
+        def radiance(g, h):
+            for k in (2 * h, 2 * h + 1):
+                cols = slice(128 * k, 128 * k + 128)
+                b = bank("fin")
+                for j in range(4):
+                    product(b[:, 128 * j : 128 * j + 128], "the", g, j, "l", cols)
+                nc.scalar.copy(out=rt[g][:, cols, :], in_=b[:].rearrange("p (j n) -> p n j", j=4))
+
+        def quant_rad(g):
+            nc.vector.quantize_mx(
+                out=rq[g][:].bitcast(FP8X4), scales=rs[g][:], in_=rt[g][:].rearrange("p n j -> p (n j)")
+            )
+
+        res = {c: keep.tile([128, 4, N], F32, name=f"res{c}", align_bytes=64) for c in range(2)}
+        ob = {c: keep.tile([128, N, 4], BF16, name=f"ob{c}", align_bytes=64) for c in range(2)}
+        oq = {c: keep.tile([128, N], U32, name=f"oq{c}", align_bytes=64) for c in range(2)}
+        osc = {c: keep.tile([128, N], U8, name=f"osc{c}", align_bytes=64) for c in range(2)}
+
+        def transport(b, c, t, g, start, stop):
+            nc.tensor.matmul_mx(
+                out=b[:],
+                lhsT=tq[c, g][:, 128 * t : 128 * t + 128].bitcast(FP8X4),
+                lhsT_scale=ts[c, g][:, 128 * t : 128 * t + 128],
+                rhs=rq[g][:].bitcast(FP8X4),
+                rhs_scale=rs[g][:],
+                start=start,
+                stop=stop,
+            )
+
+        def result(b, c, t, eng):
+            if eng == "S":
+                nc.scalar.activation(out=res[c][:, t, :], in_=b[:], func=COPY, scale=COEF)
+            else:
+                nc.vector.tensor_scalar(out=res[c][:, t, :], in0=b[:], scalar1=COEF, scalar2=None, op0=MULT)
+            if t % 2 == 1:
+                rows = out_0[512 * c : 512 * c + 512, :].rearrange("(p t) n -> p t n", t=4)
+                nc.sync.dma_start(out=rows[:, t - 1 : t + 1, :], in_=res[c][:, t - 1 : t + 1, :])
+
+        def final0(h, engs):
+            for i in range(2):
+                t = 2 * h + i
+                b = bank("fin")
+                transport(b, 0, t, 0, True, False)
+                transport(b, 0, t, 1, False, True)
+                result(b, 0, t, engs[i])
+
+        tail = {}
+
+        def open_final1():
+            for t in range(4):
+                tail[t] = bank("fin" if t < 2 else "tp")
+                transport(tail[t], 1, t, 0, True, False)
+
+        def close_final1(h, engs):
+            for i in range(2):
+                t = 2 * h + i
+                transport(tail[t], 1, t, 1, False, True)
+                result(tail[t], 1, t, engs[i])
+
+        def regroup(c, h, eng):
+            cols = slice(256 * h, 256 * h + 256)
+            src = res[c][:, :, cols].rearrange("p t n -> p n t")
+            if eng == "S":
+                nc.scalar.copy(out=ob[c][:, cols, :], in_=src)
+            else:
+                nc.vector.tensor_copy(out=ob[c][:, cols, :], in_=src)
+
+        planes_done = {0: [], 1: []}
+
+        def quant_out(c, h):
+            cols = slice(256 * h, 256 * h + 256)
+            nc.vector.quantize_mx(
+                out=oq[c][:, cols].bitcast(FP8X4),
+                scales=osc[c][:, cols],
+                in_=ob[c][:, cols, :].rearrange("p n t -> p (n t)"),
+            )
+            nc.sync.dma_start(
+                out=out_1[c].rearrange("p m t -> p (m t)")[:, 1024 * h : 1024 * h + 1024].bitcast(I32),
+                in_=oq[c][:, cols].bitcast(I32),
+            )
+            planes_done[c].append(h)
+            if len(planes_done[c]) == 2:
+                for s in range(4):
+                    nc.sync.dma_start(
+                        out=out_2[c, 4 * s : 4 * s + 4, :].bitcast(I32), in_=osc[c][32 * s : 32 * s + 4, :].bitcast(I32)
+                    )
+
+        for h in range(2):
+            turn("v0", h, "S")
+        order_scales(psi_s, psi_s_raw)
+        order_words("psi", 0)
+        quant("v0")
+        for h in range(2):
+            turn("r0", h, "V")
+        order_words("psi", 1)
+        quant("r0")
+        visible(0, 0, 0)
+        order_scales(pt_s, pt_s_raw)
+        order_words("phi", 0)
+        order_words("phi", 1)
+        visible(0, 1, 0)
+        order_words("the", 0)
+        order_words("the", 1)
+        for h in range(2):
+            turn("l", h, "S")
+        reflect(0, 0, 0)
+        visible(0, 0, 1)
+        quant("l")
+        reflect(0, 0, 1)
+        for h in range(2):
+            turn("v1", h, "S")
+        visible(0, 1, 1)
+        interleave(0, 0, ALL, "V")
+        for h in range(2):
+            turn("r1", h, "S")
+        quant("v1")
+        quant_tr(0, 0, ALL)
+        reflect(0, 1, 0)
+        visible(1, 0, 0)
+        quant("r1")
+        radiance(0, 0)
+        visible(1, 1, 0)
+        reflect(0, 1, 1)
+        radiance(0, 1)
+        interleave(0, 1, ALL, "V")
+        visible(1, 0, 1)
+        reflect(1, 0, 0)
+        radiance(1, 0)
+        visible(1, 1, 1)
+        quant_tr(0, 1, ALL)
+        quant_rad(0)
+        radiance(1, 1)
+        reflect(1, 0, 1)
+        interleave(1, 0, ALL, "S")
+        reflect(1, 1, 0)
+        quant_rad(1)
+        reflect(1, 1, 1)
+        quant_tr(1, 0, ALL)
+        halves = (slice(0, 256), slice(256, 512))
+        for cols in halves:
+            interleave(1, 1, cols, "V")
+        for h in range(2):
+            final0(h, "SS")
+        quant_tr(1, 1, halves[0])
+        regroup(0, 0, "V")
+        quant_tr(1, 1, halves[1])
+        quant_out(0, 0)
+        regroup(0, 1, "S")
+        quant_out(0, 1)
+        open_final1()
+        close_final1(0, "SS")
+        close_final1(1, "VS")
+        regroup(1, 1, "S")
+        regroup(1, 0, "V")
+        quant_out(1, 0)
+        quant_out(1, 1)

@@ -38,9 +38,9 @@ def tile_tripleproductvisibilityreflectancereligh_x2_kernel(
                 )
                 x_raw[name, h] = t
 
-        def load_scales(dst, k, src):
+        def load_scales(queue, dst, k, src):
             for s in range(4):
-                nc.sync.dma_start(
+                queue.dma_start(
                     out=dst[32 * s + k : 32 * s + k + 4, :].bitcast(I32), in_=src[0, 4 * s : 4 * s + 4, :].bitcast(I32)
                 )
 
@@ -55,6 +55,7 @@ def tile_tripleproductvisibilityreflectancereligh_x2_kernel(
         pt_s_raw = keep.tile([128, W], U8, name="pt_s_raw", align_bytes=64)
         nc.vector.memset(psi_s_raw[:].bitcast(I32), 0)
         nc.vector.memset(pt_s_raw[:].bitcast(I32), 0)
+        load_scales(nc.scalar, psi_s_raw, 0, psi_scales)
         ident = keep.tile([128, 128], F32, name="ident", align_bytes=64)
         make_identity(nc, ident[:])
         warm = keep.tile([128, 1], F32, name="warm")
@@ -65,11 +66,10 @@ def tile_tripleproductvisibilityreflectancereligh_x2_kernel(
         nc.gpsimd.dma_start(out=q_sb[:], in_=q.rearrange("(g p t) -> p g t", g=2, t=4))
 
         load_rows("v0", v, 0)
-        load_scales(psi_s_raw, 0, psi_scales)
         load_words("psi", psi_words)
         load_rows("r0", r, 0)
-        load_scales(pt_s_raw, 0, phi_scales)
-        load_scales(pt_s_raw, 4, theta_scales)
+        load_scales(nc.sync, pt_s_raw, 0, phi_scales)
+        load_scales(nc.sync, pt_s_raw, 4, theta_scales)
         load_words("phi", phi_words)
         load_rows("l", l, 0, "(t p) k -> p t k")
         load_words("the", theta_words)
@@ -92,7 +92,7 @@ def tile_tripleproductvisibilityreflectancereligh_x2_kernel(
                     )
             if h == 0 or name not in xt:
                 if name not in xt:
-                    xt[name] = work.tile([128, 512, 4], BF16, name="xt", align_bytes=64)
+                    xt[name] = work.tile([128, 512, 4], BF16, name="xt", bufs=3, align_bytes=64)
             dst = (
                 xt[name][:, 256 * h : 256 * h + 256, :]
                 .rearrange("p n t -> p (n t)")
@@ -164,6 +164,16 @@ def tile_tripleproductvisibilityreflectancereligh_x2_kernel(
                     out=tr[c, g][:, j, :], in0=b[:], scalar=q_sb[:, g, j : j + 1], in1=vis[c, g, j][:], op0=MULT, op1=MULT
                 )
 
+        def reflect_columns(c, g, cols):
+            if (c, g) not in tr:
+                tr[c, g] = work.tile([128, 4, 512], BF16, name="tr", bufs=3, align_bytes=64)
+            for j in range(4):
+                b = bank("ref")
+                product(b[:, 0:256], "phi", g, j, f"r{c}", cols)
+                nc.vector.scalar_tensor_tensor(
+                    out=tr[c, g][:, j, cols], in0=b[:, 0:256], scalar=q_sb[:, g, j : j + 1], in1=vis[c, g, j][:, cols], op0=MULT, op1=MULT
+                )
+
         def interleave(c, g, cols, eng):
             if (c, g) not in ti:
                 ti[c, g] = work.tile([128, 512, 4], BF16, name="ti", bufs=3, align_bytes=64)
@@ -188,13 +198,17 @@ def tile_tripleproductvisibilityreflectancereligh_x2_kernel(
         rq = {g: keep.tile([128, N], U32, name=f"rq{g}", align_bytes=64) for g in range(2)}
         rs = {g: keep.tile([128, N], U8, name=f"rs{g}", align_bytes=64) for g in range(2)}
 
-        def radiance(g, h):
+        def radiance(g, h, engs="SS"):
             for k in (2 * h, 2 * h + 1):
                 cols = slice(128 * k, 128 * k + 128)
                 b = bank("fin")
                 for j in range(4):
                     product(b[:, 128 * j : 128 * j + 128], "the", g, j, "l", cols)
-                nc.scalar.copy(out=rt[g][:, cols, :], in_=b[:].rearrange("p (j n) -> p n j", j=4))
+                src = b[:].rearrange("p (j n) -> p n j", j=4)
+                if engs[k % 2] == "S":
+                    nc.scalar.copy(out=rt[g][:, cols, :], in_=src)
+                else:
+                    nc.vector.tensor_copy(out=rt[g][:, cols, :], in_=src)
 
         def quant_rad(g):
             nc.vector.quantize_mx(
@@ -275,72 +289,75 @@ def tile_tripleproductvisibilityreflectancereligh_x2_kernel(
                         out=out_2[c, 4 * s : 4 * s + 4, :].bitcast(I32), in_=osc[c][32 * s : 32 * s + 4, :].bitcast(I32)
                     )
 
-        for h in range(2):
-            turn("v0", h, "S")
+        halves = (slice(0, 256), slice(256, 512))
         order_scales(psi_s, psi_s_raw)
         order_words("psi", 0)
+        turn("v0", 0, "V")
+        turn("v0", 1, "S")
         quant("v0")
-        for h in range(2):
-            turn("r0", h, "V")
+        turn("r0", 0, "V")
+        turn("r0", 1, "S")
         order_words("psi", 1)
-        quant("r0")
         visible(0, 0, 0)
-        order_scales(pt_s, pt_s_raw)
         order_words("phi", 0)
+        order_scales(pt_s, pt_s_raw)
         order_words("phi", 1)
-        visible(0, 1, 0)
-        order_words("the", 0)
-        order_words("the", 1)
-        for h in range(2):
-            turn("l", h, "S")
-        reflect(0, 0, 0)
+        turn("l", 0, "S")
+        turn("l", 1, "S")
         visible(0, 0, 1)
+        quant("r0")
+        order_words("the", 0)
+        reflect(0, 0, 0)
+        turn("v1", 0, "S")
+        turn("v1", 1, "S")
         quant("l")
+        order_words("the", 1)
         reflect(0, 0, 1)
-        for h in range(2):
-            turn("v1", h, "S")
-        visible(0, 1, 1)
-        interleave(0, 0, ALL, "V")
-        for h in range(2):
-            turn("r1", h, "S")
+        visible(0, 1, 0)
         quant("v1")
-        quant_tr(0, 0, ALL)
+        radiance(0, 0, "SS")
+        interleave(0, 0, halves[0], "V")
+        interleave(0, 0, halves[1], "V")
+        turn("r1", 0, "S")
+        turn("r1", 1, "V")
+        visible(0, 1, 1)
         reflect(0, 1, 0)
+        radiance(1, 0, "SS")
         visible(1, 0, 0)
-        quant("r1")
-        radiance(0, 0)
-        visible(1, 1, 0)
+        quant_tr(0, 0, ALL)
         reflect(0, 1, 1)
-        radiance(0, 1)
-        interleave(0, 1, ALL, "V")
+        radiance(0, 1, "VS")
+        quant("r1")
         visible(1, 0, 1)
+        quant_rad(0)
+        interleave(0, 1, halves[0], "V")
+        radiance(1, 1, "SS")
         reflect(1, 0, 0)
-        radiance(1, 0)
+        visible(1, 1, 0)
+        interleave(0, 1, halves[1], "S")
+        quant_rad(1)
+        reflect(1, 0, 1)
         visible(1, 1, 1)
         quant_tr(0, 1, ALL)
-        quant_rad(0)
-        radiance(1, 1)
-        reflect(1, 0, 1)
-        interleave(1, 0, ALL, "S")
-        reflect(1, 1, 0)
-        quant_rad(1)
-        reflect(1, 1, 1)
+        reflect_columns(1, 1, halves[0])
+        interleave(1, 0, halves[0], "S")
+        interleave(1, 0, halves[1], "V")
+        final0(0, "SS")
+        reflect_columns(1, 1, halves[1])
+        interleave(1, 1, halves[0], "S")
         quant_tr(1, 0, ALL)
-        halves = (slice(0, 256), slice(256, 512))
-        for cols in halves:
-            interleave(1, 1, cols, "V")
-        for h in range(2):
-            final0(h, "SS")
+        final0(1, "SS")
+        regroup(0, 0, "S")
         quant_tr(1, 1, halves[0])
-        regroup(0, 0, "V")
-        quant_tr(1, 1, halves[1])
-        quant_out(0, 0)
-        regroup(0, 1, "S")
-        quant_out(0, 1)
         open_final1()
-        close_final1(0, "SS")
+        interleave(1, 1, halves[1], "V")
+        regroup(0, 1, "V")
+        quant_tr(1, 1, halves[1])
+        quant_out(0, 1)
+        quant_out(0, 0)
+        close_final1(0, "SV")
         close_final1(1, "VS")
-        regroup(1, 1, "S")
-        regroup(1, 0, "V")
-        quant_out(1, 0)
+        regroup(1, 1, "V")
+        regroup(1, 0, "S")
         quant_out(1, 1)
+        quant_out(1, 0)

@@ -12,6 +12,7 @@ FP8X4 = mybir.dt.float8_e4m3fn_x4
 COPY = mybir.ActivationFunctionType.Copy
 SIGMOID = mybir.ActivationFunctionType.Sigmoid
 MULT = mybir.AluOpType.mult
+ADD = mybir.AluOpType.add
 
 P, K, W, N = 1024, 512, 1024, 512
 FLOPS = 2 * (2 * P * K * W + N * K * W + P * W * N)
@@ -30,32 +31,30 @@ def tile_tripleproductvisibilityreflectancereligh_x2_kernel(
     ):
         x_raw = {}
 
-        def load_rows(name, src, c, order="(p t) k -> p t k"):
+        def load_rows(name, src, c, order="(p t) k -> p t k", parts=1):
+            rows = src[512 * c : 512 * c + 512, :].rearrange(order, t=4)
+            t = keep.tile([128, 4, K], BF16, name=f"{name}_raw", align_bytes=64)
             for h in range(2):
-                t = keep.tile([128, 2, K], BF16, name=f"{name}_raw{h}", align_bytes=64)
-                nc.sync.dma_start(
-                    out=t[:], in_=src[512 * c : 512 * c + 512, :].rearrange(order, t=4)[:, 2 * h : 2 * h + 2, :]
-                )
-                x_raw[name, h] = t
+                x_raw[name, h] = t[:, 2 * h : 2 * h + 2, :]
+            return t, rows
 
-        def load_scales(queue, dst, k, src):
+        def load_scales(queue, dst, src):
             for s in range(4):
                 queue.dma_start(
-                    out=dst[32 * s + k : 32 * s + k + 4, :].bitcast(I32), in_=src[0, 4 * s : 4 * s + 4, :].bitcast(I32)
+                    out=dst[32 * s : 32 * s + 4, :].bitcast(I32), in_=src[0, 4 * s : 4 * s + 4, :].bitcast(I32)
                 )
 
-        w_raw = {}
+        w_raw, s_raw = {}, {}
 
         def load_words(name, src):
             t = keep.tile([128, W], U32, name=f"{name}_raw", align_bytes=64)
             nc.sync.dma_start(out=t[:].bitcast(I32), in_=src[0].rearrange("p n t -> p (n t)").bitcast(I32))
             w_raw[name] = t
 
-        psi_s_raw = keep.tile([128, W], U8, name="psi_s_raw", align_bytes=64)
-        pt_s_raw = keep.tile([128, W], U8, name="pt_s_raw", align_bytes=64)
-        nc.vector.memset(psi_s_raw[:].bitcast(I32), 0)
-        nc.vector.memset(pt_s_raw[:].bitcast(I32), 0)
-        load_scales(nc.scalar, psi_s_raw, 0, psi_scales)
+        for name in ("psi", "phi", "the"):
+            s_raw[name] = keep.tile([128, W], U8, name=f"{name}_s_raw", align_bytes=64)
+            (nc.gpsimd if name == "psi" else nc.vector).memset(s_raw[name][:].bitcast(I32), 0)
+        load_scales(nc.scalar, s_raw["psi"], psi_scales)
         ident = keep.tile([128, 128], F32, name="ident", align_bytes=64)
         make_identity(nc, ident[:])
         warm = keep.tile([128, 1], F32, name="warm")
@@ -65,16 +64,24 @@ def tile_tripleproductvisibilityreflectancereligh_x2_kernel(
         q_sb = keep.tile([128, 2, 4], BF16, name="q_sb")
         nc.gpsimd.dma_start(out=q_sb[:], in_=q.rearrange("(g p t) -> p g t", g=2, t=4))
 
-        load_rows("v0", v, 0)
+        v0_t, v0_rows = load_rows("v0", v, 0)
+        r0_t, r0_rows = load_rows("r0", r, 0)
+        l_t, l_rows = load_rows("l", l, 0, "(t p) k -> p t k")
+        v1_t, v1_rows = load_rows("v1", v, 1)
+        r1_t, r1_rows = load_rows("r1", r, 1)
+        ONE, TWO = slice(0, 2), slice(2, 4)
+        nc.sync.dma_start(out=v0_t[:, ONE, :], in_=v0_rows[:, ONE, :])
         load_words("psi", psi_words)
-        load_rows("r0", r, 0)
-        load_scales(nc.sync, pt_s_raw, 0, phi_scales)
-        load_scales(nc.sync, pt_s_raw, 4, theta_scales)
+        nc.sync.dma_start(out=v0_t[:, TWO, :], in_=v0_rows[:, TWO, :])
+        nc.sync.dma_start(out=r0_t[:, ONE, :], in_=r0_rows[:, ONE, :])
+        load_scales(nc.sync, s_raw["phi"], phi_scales)
+        nc.sync.dma_start(out=r0_t[:, TWO, :], in_=r0_rows[:, TWO, :])
         load_words("phi", phi_words)
-        load_rows("l", l, 0, "(t p) k -> p t k")
+        nc.sync.dma_start(out=l_t[:], in_=l_rows)
         load_words("the", theta_words)
-        load_rows("v1", v, 1)
-        load_rows("r1", r, 1)
+        load_scales(nc.sync, s_raw["the"], theta_scales)
+        nc.sync.dma_start(out=v1_t[:], in_=v1_rows)
+        nc.sync.dma_start(out=r1_t[:], in_=r1_rows)
 
         xt, xq, xs = {}, {}, {}
 
@@ -83,45 +90,39 @@ def tile_tripleproductvisibilityreflectancereligh_x2_kernel(
             return t
 
         def turn(name, h, eng):
-            words = x_raw[name, h][:].rearrange("p t k -> p (t k)").bitcast(F32)
+            words = x_raw[name, h].rearrange("p t k -> p (t k)").bitcast(F32)
             b = bank("tp")
             for a in range(2):
                 for u in range(2):
                     nc.tensor.transpose(
                         b[:, 256 * a + 128 * u : 256 * a + 128 * u + 128], words[:, 256 * a + u : 256 * (a + 1) : 2], ident[:]
                     )
-            if h == 0 or name not in xt:
-                if name not in xt:
-                    xt[name] = work.tile([128, 512, 4], BF16, name="xt", bufs=3, align_bytes=64)
-            dst = (
-                xt[name][:, 256 * h : 256 * h + 256, :]
-                .rearrange("p n t -> p (n t)")
-                .bitcast(F32)
-                .rearrange("p (a r u) -> p a r u", a=2, u=2)
-            )
+            xt[name, h] = work.tile([128, 256, 4], BF16, name="xt", bufs=6, align_bytes=64)
+            dst = xt[name, h][:].rearrange("p n t -> p (n t)").bitcast(F32).rearrange("p (a r u) -> p a r u", a=2, u=2)
             src = b[:].rearrange("p (a u r) -> p a r u", a=2, u=2)
             if eng == "S":
                 nc.scalar.copy(out=dst, in_=src)
             else:
                 nc.vector.tensor_copy(out=dst, in_=src)
 
-        def quant(name):
-            xq[name] = keep.tile([128, 512], U32, name=f"{name}_q", align_bytes=64)
-            xs[name] = keep.tile([128, 512], U8, name=f"{name}_s", align_bytes=64)
+        def quant(name, h):
+            if name not in xq:
+                xq[name] = keep.tile([128, 512], U32, name=f"{name}_q", align_bytes=64)
+                xs[name] = keep.tile([128, 512], U8, name=f"{name}_s", align_bytes=64)
+            cols = slice(256 * h, 256 * h + 256)
             nc.vector.quantize_mx(
-                out=xq[name][:].bitcast(FP8X4), scales=xs[name][:], in_=xt[name][:].rearrange("p n t -> p (n t)")
+                out=xq[name][:, cols].bitcast(FP8X4),
+                scales=xs[name][:, cols],
+                in_=xt[name, h][:].rearrange("p n t -> p (n t)"),
             )
 
         wp = {n: keep.tile([128, W], U32, name=f"{n}_p", align_bytes=64) for n in ("psi", "phi", "the")}
-        psi_s = keep.tile([128, W], U8, name="psi_s", align_bytes=64)
-        pt_s = keep.tile([128, W], U8, name="pt_s", align_bytes=64)
+        ws = {n: keep.tile([128, W], U8, name=f"{n}_s", align_bytes=64) for n in ("psi", "phi", "the")}
 
-        def scale_plane(name):
-            return {"psi": (psi_s, 0), "phi": (pt_s, 0), "the": (pt_s, 4)}[name]
-
-        def order_scales(dst, src):
+        def order_scales(name):
             nc.vector.tensor_copy(
-                out=dst[:].rearrange("p (g j m) -> p g m j", g=2, j=4), in_=src[:].rearrange("p (g m j) -> p g m j", g=2, j=4)
+                out=ws[name][:].rearrange("p (g j m) -> p g m j", g=2, j=4),
+                in_=s_raw[name][:].rearrange("p (g m j) -> p g m j", g=2, j=4),
             )
 
         def order_words(name, g):
@@ -133,56 +134,55 @@ def tile_tripleproductvisibilityreflectancereligh_x2_kernel(
 
         def product(dst, name, g, j, x, cols):
             c0 = 512 * g + 128 * j
-            plane, k = scale_plane(name)
             nc.tensor.matmul_mx(
                 out=dst,
                 lhsT=wp[name][:, c0 : c0 + 128].bitcast(FP8X4),
-                lhsT_scale=plane[k:128, c0 : c0 + 128],
+                lhsT_scale=ws[name][:, c0 : c0 + 128],
                 rhs=xq[x][:, cols].bitcast(FP8X4),
                 rhs_scale=xs[x][:, cols],
                 start=True,
                 stop=True,
             )
 
-        vis, tr, ti, tq, ts = {}, {}, {}, {}, {}
-        ALL = slice(0, 512)
+        vs, vq, ti, tq, ts = {}, {}, {}, {}, {}
+        halves = (slice(0, 256), slice(256, 512))
 
         def visible(c, g, h):
-            for j in (2 * h, 2 * h + 1):
+            if (c, g) not in vs:
+                vs[c, g] = work.tile([128, 4, 512], F32, name="vs", bufs=3, align_bytes=64)
+            for jp in (0, 2):
                 b = bank("vis")
-                product(b[:], "psi", g, j, f"v{c}", ALL)
-                vis[c, g, j] = work.tile([128, 512], F32, name="vs", bufs=8, align_bytes=64)
-                nc.scalar.activation(out=vis[c, g, j][:], in_=b[:], func=SIGMOID)
+                for i in range(2):
+                    product(b[:, 256 * i : 256 * i + 256], "psi", g, jp + i, f"v{c}", halves[h])
+                nc.scalar.activation(
+                    out=vs[c, g][:, jp : jp + 2, halves[h]], in_=b[:].rearrange("p (j n) -> p j n", j=2), func=SIGMOID
+                )
+
+        def weigh(c, g, jp, engs):
+            if (c, g) not in vq:
+                vq[c, g] = work.tile([128, 4, 512], F32, name="vq", bufs=3, align_bytes=64)
+            for i in range(2):
+                j = 2 * jp + i
+                src, dst, scalar = vs[c, g][:, j, :], vq[c, g][:, j, :], q_sb[:, g, j : j + 1]
+                if engs[i] == "V":
+                    nc.vector.tensor_scalar(out=dst, in0=src, scalar1=scalar, scalar2=None, op0=MULT)
+                else:
+                    nc.gpsimd.tensor_scalar(out=dst, in0=src, scalar1=scalar, scalar2=0.0, op0=MULT, op1=ADD)
 
         def reflect(c, g, h):
-            if (c, g) not in tr:
-                tr[c, g] = work.tile([128, 4, 512], BF16, name="tr", bufs=3, align_bytes=64)
-            for j in (2 * h, 2 * h + 1):
-                b = bank("ref")
-                product(b[:], "phi", g, j, f"r{c}", ALL)
-                nc.vector.scalar_tensor_tensor(
-                    out=tr[c, g][:, j, :], in0=b[:], scalar=q_sb[:, g, j : j + 1], in1=vis[c, g, j][:], op0=MULT, op1=MULT
-                )
-
-        def reflect_columns(c, g, cols):
-            if (c, g) not in tr:
-                tr[c, g] = work.tile([128, 4, 512], BF16, name="tr", bufs=3, align_bytes=64)
-            for j in range(4):
-                b = bank("ref")
-                product(b[:, 0:256], "phi", g, j, f"r{c}", cols)
-                nc.vector.scalar_tensor_tensor(
-                    out=tr[c, g][:, j, cols], in0=b[:, 0:256], scalar=q_sb[:, g, j : j + 1], in1=vis[c, g, j][:, cols], op0=MULT, op1=MULT
-                )
-
-        def interleave(c, g, cols, eng):
-            if (c, g) not in ti:
+            if h == 0:
                 ti[c, g] = work.tile([128, 512, 4], BF16, name="ti", bufs=3, align_bytes=64)
-            dst = ti[c, g][:, cols, :]
-            src = tr[c, g][:, :, cols].rearrange("p j n -> p n j")
-            if eng == "S":
-                nc.scalar.copy(out=dst, in_=src)
-            else:
-                nc.vector.tensor_copy(out=dst, in_=src)
+            for k in (2 * h, 2 * h + 1):
+                cols = slice(128 * k, 128 * k + 128)
+                b = bank("ref")
+                for j in range(4):
+                    product(b[:, 128 * j : 128 * j + 128], "phi", g, j, f"r{c}", cols)
+                nc.vector.tensor_tensor(
+                    out=ti[c, g][:, cols, :],
+                    in0=b[:].rearrange("p (j n) -> p n j", j=4),
+                    in1=vq[c, g][:, :, cols].rearrange("p j n -> p n j"),
+                    op=MULT,
+                )
 
         def quant_tr(c, g, cols):
             if (c, g) not in tq:
@@ -218,7 +218,7 @@ def tile_tripleproductvisibilityreflectancereligh_x2_kernel(
         res = {c: keep.tile([128, 4, N], F32, name=f"res{c}", align_bytes=64) for c in range(2)}
         ob = {c: keep.tile([128, N, 4], BF16, name=f"ob{c}", align_bytes=64) for c in range(2)}
         oq = {c: keep.tile([128, N], U32, name=f"oq{c}", align_bytes=64) for c in range(2)}
-        osc = {c: keep.tile([128, N], U8, name=f"osc{c}", align_bytes=64) for c in range(2)}
+        osc = keep.tile([128, 2, N], U8, name="osc", align_bytes=64)
 
         def transport(b, c, t, g, start, stop):
             nc.tensor.matmul_mx(
@@ -275,89 +275,103 @@ def tile_tripleproductvisibilityreflectancereligh_x2_kernel(
             cols = slice(256 * h, 256 * h + 256)
             nc.vector.quantize_mx(
                 out=oq[c][:, cols].bitcast(FP8X4),
-                scales=osc[c][:, cols],
+                scales=osc[:, c, cols],
                 in_=ob[c][:, cols, :].rearrange("p n t -> p (n t)"),
             )
-            nc.sync.dma_start(
-                out=out_1[c].rearrange("p m t -> p (m t)")[:, 1024 * h : 1024 * h + 1024].bitcast(I32),
-                in_=oq[c][:, cols].bitcast(I32),
-            )
             planes_done[c].append(h)
-            if len(planes_done[c]) == 2:
-                for s in range(4):
-                    nc.sync.dma_start(
-                        out=out_2[c, 4 * s : 4 * s + 4, :].bitcast(I32), in_=osc[c][32 * s : 32 * s + 4, :].bitcast(I32)
-                    )
+            words = out_1[c].rearrange("p m t -> p (m t)")
+            if c == 1:
+                nc.sync.dma_start(
+                    out=words[:, 1024 * h : 1024 * h + 1024].bitcast(I32), in_=oq[c][:, cols].bitcast(I32)
+                )
+            elif len(planes_done[c]) == 2:
+                nc.sync.dma_start(out=words.bitcast(I32), in_=oq[c][:].bitcast(I32))
 
-        halves = (slice(0, 256), slice(256, 512))
-        order_scales(psi_s, psi_s_raw)
+        def store_scales():
+            for s in range(4):
+                nc.sync.dma_start(
+                    out=out_2[:, 4 * s : 4 * s + 4, :].rearrange("c s m -> s c m").bitcast(I32),
+                    in_=osc[32 * s : 32 * s + 4, :, :].bitcast(I32),
+                )
+
+        order_scales("psi")
         order_words("psi", 0)
-        turn("v0", 0, "V")
+        turn("v0", 0, "S")
+        quant("v0", 0)
         turn("v0", 1, "S")
-        quant("v0")
-        turn("r0", 0, "V")
-        turn("r0", 1, "S")
-        order_words("psi", 1)
         visible(0, 0, 0)
+        turn("r0", 0, "S")
+        quant("v0", 1)
+        order_words("psi", 1)
+        order_scales("phi")
         order_words("phi", 0)
-        order_scales(pt_s, pt_s_raw)
         order_words("phi", 1)
-        turn("l", 0, "S")
-        turn("l", 1, "S")
+        quant("r0", 0)
         visible(0, 0, 1)
-        quant("r0")
-        order_words("the", 0)
-        reflect(0, 0, 0)
-        turn("v1", 0, "S")
-        turn("v1", 1, "S")
-        quant("l")
-        order_words("the", 1)
-        reflect(0, 0, 1)
+        turn("l", 0, "V")
+        turn("r0", 1, "S")
+        weigh(0, 0, 0, "GV")
+        weigh(0, 0, 1, "VV")
         visible(0, 1, 0)
-        quant("v1")
-        radiance(0, 0, "SS")
-        interleave(0, 0, halves[0], "V")
-        interleave(0, 0, halves[1], "V")
-        turn("r1", 0, "S")
-        turn("r1", 1, "V")
+        order_scales("the")
+        order_words("the", 0)
+        quant("r0", 1)
+        quant("l", 0)
+        turn("l", 1, "S")
+        turn("v1", 0, "S")
+        order_words("the", 1)
         visible(0, 1, 1)
-        reflect(0, 1, 0)
-        radiance(1, 0, "SS")
+        quant("v1", 0)
+        reflect(0, 0, 0)
+        weigh(0, 1, 0, "GG")
+        turn("v1", 1, "S")
+        turn("r1", 0, "V")
+        quant("v1", 1)
         visible(1, 0, 0)
-        quant_tr(0, 0, ALL)
-        reflect(0, 1, 1)
-        radiance(0, 1, "VS")
-        quant("r1")
+        reflect(0, 0, 1)
+        radiance(0, 0, "SS")
+        weigh(0, 1, 1, "GG")
         visible(1, 0, 1)
-        quant_rad(0)
-        interleave(0, 1, halves[0], "V")
-        radiance(1, 1, "SS")
-        reflect(1, 0, 0)
+        quant("l", 1)
+        radiance(1, 0, "SS")
+        quant_tr(0, 0, halves[0])
+        quant("r1", 0)
+        weigh(1, 0, 0, "GG")
+        reflect(0, 1, 0)
+        turn("r1", 1, "V")
         visible(1, 1, 0)
-        interleave(0, 1, halves[1], "S")
-        quant_rad(1)
-        reflect(1, 0, 1)
+        quant_tr(0, 0, halves[1])
+        weigh(1, 0, 1, "GG")
+        reflect(0, 1, 1)
+        radiance(0, 1, "SS")
+        quant("r1", 1)
+        quant_tr(0, 1, halves[0])
         visible(1, 1, 1)
-        quant_tr(0, 1, ALL)
-        reflect_columns(1, 1, halves[0])
-        interleave(1, 0, halves[0], "S")
-        interleave(1, 0, halves[1], "V")
+        quant_rad(0)
+        radiance(1, 1, "SS")
+        weigh(1, 1, 0, "GG")
+        reflect(1, 0, 0)
+        quant_rad(1)
+        weigh(1, 1, 1, "GG")
+        reflect(1, 0, 1)
         final0(0, "SS")
-        reflect_columns(1, 1, halves[1])
-        interleave(1, 1, halves[0], "S")
-        quant_tr(1, 0, ALL)
-        final0(1, "SS")
-        regroup(0, 0, "S")
+        quant_tr(0, 1, halves[1])
+        quant_tr(1, 0, halves[0])
+        reflect(1, 1, 0)
+        quant_tr(1, 0, halves[1])
         quant_tr(1, 1, halves[0])
+        final0(1, "SS")
+        regroup(0, 1, "S")
+        reflect(1, 1, 1)
+        regroup(0, 0, "V")
         open_final1()
-        interleave(1, 1, halves[1], "V")
-        regroup(0, 1, "V")
+        close_final1(0, "SS")
         quant_tr(1, 1, halves[1])
         quant_out(0, 1)
         quant_out(0, 0)
-        close_final1(0, "SV")
         close_final1(1, "VS")
-        regroup(1, 1, "V")
         regroup(1, 0, "S")
+        regroup(1, 1, "V")
         quant_out(1, 1)
         quant_out(1, 0)
+        store_scales()

@@ -178,9 +178,9 @@ def tile_tripleproductvisibilityreflectancereligh_x2_kernel(
                 for j in range(4):
                     product(b[:, 128 * j : 128 * j + 128], "phi", g, j, f"r{c}", cols)
                 nc.vector.tensor_tensor(
-                    out=ti[c, g][:, cols, :],
-                    in0=b[:].rearrange("p (j n) -> p n j", j=4),
-                    in1=vq[c, g][:, :, cols].rearrange("p j n -> p n j"),
+                    out=ti[c, g][:, cols, :].rearrange("p (c i) j -> p c j i", i=4),
+                    in0=b[:].rearrange("p (j c i) -> p c j i", j=4, i=4),
+                    in1=vq[c, g][:, :, cols].rearrange("p j (c i) -> p c j i", i=4),
                     op=MULT,
                 )
 
@@ -263,11 +263,12 @@ def tile_tripleproductvisibilityreflectancereligh_x2_kernel(
 
         def regroup(c, h, eng):
             cols = slice(256 * h, 256 * h + 256)
-            src = res[c][:, :, cols].rearrange("p t n -> p n t")
+            src = res[c][:, :, cols].rearrange("p t (d i) -> p d t i", i=4)
+            dst = ob[c][:, cols, :].rearrange("p (d i) t -> p d t i", i=4)
             if eng == "S":
-                nc.scalar.copy(out=ob[c][:, cols, :], in_=src)
+                nc.scalar.copy(out=dst, in_=src)
             else:
-                nc.vector.tensor_copy(out=ob[c][:, cols, :], in_=src)
+                nc.vector.tensor_copy(out=dst, in_=src)
 
         planes_done = {0: [], 1: []}
 
@@ -294,84 +295,84 @@ def tile_tripleproductvisibilityreflectancereligh_x2_kernel(
                     in_=osc[32 * s : 32 * s + 4, :, :].bitcast(I32),
                 )
 
-        order_scales("psi")
         order_words("psi", 0)
+        order_scales("psi")
         turn("v0", 0, "S")
         quant("v0", 0)
-        turn("v0", 1, "S")
-        visible(0, 0, 0)
-        turn("r0", 0, "S")
-        quant("v0", 1)
+        turn("v0", 1, "V")
         order_words("psi", 1)
-        order_scales("phi")
+        quant("v0", 1)
+        visible(0, 0, 0)
         order_words("phi", 0)
+        turn("r0", 0, "S")
         order_words("phi", 1)
+        turn("r0", 1, "V")
         quant("r0", 0)
         visible(0, 0, 1)
         turn("l", 0, "V")
-        turn("r0", 1, "S")
-        weigh(0, 0, 0, "GV")
-        weigh(0, 0, 1, "VV")
-        visible(0, 1, 0)
-        order_scales("the")
-        order_words("the", 0)
         quant("r0", 1)
-        quant("l", 0)
+        order_scales("phi")
+        visible(0, 1, 0)
+        order_words("the", 0)
+        order_words("the", 1)
         turn("l", 1, "S")
         turn("v1", 0, "S")
-        order_words("the", 1)
-        visible(0, 1, 1)
         quant("v1", 0)
-        reflect(0, 0, 0)
-        weigh(0, 1, 0, "GG")
-        turn("v1", 1, "S")
-        turn("r1", 0, "V")
-        quant("v1", 1)
-        visible(1, 0, 0)
-        reflect(0, 0, 1)
-        radiance(0, 0, "SS")
-        weigh(0, 1, 1, "GG")
-        visible(1, 0, 1)
         quant("l", 1)
-        radiance(1, 0, "SS")
+        weigh(0, 0, 0, "GG")
+        quant("l", 0)
+        order_scales("the")
+        visible(0, 1, 1)
+        weigh(0, 0, 1, "GG")
+        reflect(0, 0, 0)
+        turn("v1", 1, "S")
+        visible(1, 0, 0)
+        quant("v1", 1)
+        radiance(0, 0, "SS")
+        reflect(0, 0, 1)
         quant_tr(0, 0, halves[0])
-        quant("r1", 0)
-        weigh(1, 0, 0, "GG")
-        reflect(0, 1, 0)
-        turn("r1", 1, "V")
-        visible(1, 1, 0)
+        weigh(0, 1, 0, "GG")
+        visible(1, 0, 1)
         quant_tr(0, 0, halves[1])
-        weigh(1, 0, 1, "GG")
-        reflect(0, 1, 1)
-        radiance(0, 1, "SS")
+        turn("r1", 0, "V")
+        turn("r1", 1, "V")
+        radiance(1, 0, "SS")
+        quant("r1", 0)
         quant("r1", 1)
-        quant_tr(0, 1, halves[0])
+        visible(1, 1, 0)
+        weigh(0, 1, 1, "GG")
+        reflect(0, 1, 0)
+        weigh(1, 0, 0, "GG")
+        weigh(1, 0, 1, "GG")
+        radiance(0, 1, "SS")
+        reflect(0, 1, 1)
         visible(1, 1, 1)
         quant_rad(0)
         radiance(1, 1, "SS")
-        weigh(1, 1, 0, "GG")
+        quant_tr(0, 1, halves[0])
         reflect(1, 0, 0)
         quant_rad(1)
-        weigh(1, 1, 1, "GG")
+        weigh(1, 1, 0, "GG")
         reflect(1, 0, 1)
-        final0(0, "SS")
         quant_tr(0, 1, halves[1])
         quant_tr(1, 0, halves[0])
+        weigh(1, 1, 1, "GG")
+        final0(0, "SS")
         reflect(1, 1, 0)
         quant_tr(1, 0, halves[1])
         quant_tr(1, 1, halves[0])
         final0(1, "SS")
-        regroup(0, 1, "S")
         reflect(1, 1, 1)
-        regroup(0, 0, "V")
         open_final1()
-        close_final1(0, "SS")
+        regroup(0, 1, "S")
         quant_tr(1, 1, halves[1])
-        quant_out(0, 1)
-        quant_out(0, 0)
+        regroup(0, 0, "V")
+        close_final1(0, "SS")
         close_final1(1, "VS")
-        regroup(1, 0, "S")
+        quant_out(0, 1)
         regroup(1, 1, "V")
+        quant_out(0, 0)
+        regroup(1, 0, "S")
         quant_out(1, 1)
         quant_out(1, 0)
         store_scales()

import math

import concourse.mybir as mybir
from concourse.masks import make_identity

F32 = mybir.dt.float32
BF16 = mybir.dt.bfloat16
I32 = mybir.dt.int32
U32 = mybir.dt.uint32
U8 = mybir.dt.uint8
FP8X4 = mybir.dt.float8_e4m3fn_x4
COPY = mybir.ActivationFunctionType.Copy
SIGMOID = mybir.ActivationFunctionType.Sigmoid
MULT = mybir.AluOpType.mult
ADD = mybir.AluOpType.add

P, K, W, N = 1024, 512, 1024, 512
FLOPS = 2 * (2 * P * K * W + N * K * W + P * W * N)
COEF = 4.0 * math.pi / W


def tile_tripleproductvisibilityreflectancereligh_x2_kernel(
    tc, v, psi_words, psi_scales, r, phi_words, phi_scales, q, l, theta_words, theta_scales, out_0, out_1, out_2
):
    nc = tc.nc
    with (
        tc.tile_pool(name="keep", bufs=1) as keep,
        tc.tile_pool(name="work", bufs=2) as work,
        tc.psum_pool(name="psum", bufs=2) as psum,
        tc.manual_schedule(),
    ):
        x_raw = {}

        def load_rows(name, src, c, order="(p t) k -> p t k", parts=1):
            rows = src[512 * c : 512 * c + 512, :].rearrange(order, t=4)
            t = keep.tile([128, 4, K], BF16, name=f"{name}_raw", align_bytes=64)
            for h in range(2):
                x_raw[name, h] = t[:, 2 * h : 2 * h + 2, :]
            return t, rows

        def load_scales(queue, dst, src):
            for s in range(4):
                queue.dma_start(
                    out=dst[32 * s : 32 * s + 4, :].bitcast(I32), in_=src[0, 4 * s : 4 * s + 4, :].bitcast(I32)
                )

        w_raw, s_raw = {}, {}

        def load_words(name, src):
            t = keep.tile([128, W], U32, name=f"{name}_raw", align_bytes=64)
            nc.sync.dma_start(out=t[:].bitcast(I32), in_=src[0].rearrange("p n t -> p (n t)").bitcast(I32))
            w_raw[name] = t

        for name in ("psi", "phi", "the"):
            s_raw[name] = keep.tile([128, W], U8, name=f"{name}_s_raw", align_bytes=64)
            (nc.gpsimd if name == "psi" else nc.vector).memset(s_raw[name][:].bitcast(I32), 0)
        load_scales(nc.scalar, s_raw["psi"], psi_scales)
        ident = keep.tile([128, 128], F32, name="ident", align_bytes=64)
        make_identity(nc, ident[:])
        warm = keep.tile([128, 1], F32, name="warm")
        nc.vector.memset(warm[:], 0.0)
        warmed = keep.tile([128, 1], F32, name="warmed")
        nc.scalar.activation(out=warmed[:], in_=warm[:], func=SIGMOID)
        q_sb = keep.tile([128, 2, 4], BF16, name="q_sb")
        nc.gpsimd.dma_start(out=q_sb[:], in_=q.rearrange("(g p t) -> p g t", g=2, t=4))

        v0_t, v0_rows = load_rows("v0", v, 0)
        r0_t, r0_rows = load_rows("r0", r, 0)
        l_t, l_rows = load_rows("l", l, 0, "(t p) k -> p t k")
        v1_t, v1_rows = load_rows("v1", v, 1)
        r1_t, r1_rows = load_rows("r1", r, 1)
        ONE, TWO = slice(0, 2), slice(2, 4)
        nc.sync.dma_start(out=v0_t[:, ONE, :], in_=v0_rows[:, ONE, :])
        load_words("psi", psi_words)
        nc.sync.dma_start(out=v0_t[:, TWO, :], in_=v0_rows[:, TWO, :])
        nc.sync.dma_start(out=r0_t[:, ONE, :], in_=r0_rows[:, ONE, :])
        load_scales(nc.sync, s_raw["phi"], phi_scales)
        nc.sync.dma_start(out=r0_t[:, TWO, :], in_=r0_rows[:, TWO, :])
        load_words("phi", phi_words)
        nc.sync.dma_start(out=l_t[:], in_=l_rows)
        load_words("the", theta_words)
        load_scales(nc.sync, s_raw["the"], theta_scales)
        nc.sync.dma_start(out=v1_t[:], in_=v1_rows)
        nc.sync.dma_start(out=r1_t[:], in_=r1_rows)

        xt, xq, xs = {}, {}, {}

        def bank(tag):
            t = psum.tile([128, 512], F32, name=tag)
            return t

        def turn(name, h, eng):
            words = x_raw[name, h].rearrange("p t k -> p (t k)").bitcast(F32)
            b = bank("tp")
            for a in range(2):
                for u in range(2):
                    nc.tensor.transpose(
                        b[:, 256 * a + 128 * u : 256 * a + 128 * u + 128], words[:, 256 * a + u : 256 * (a + 1) : 2], ident[:]
                    )
            xt[name, h] = work.tile([128, 256, 4], BF16, name="xt", bufs=6, align_bytes=64)
            dst = xt[name, h][:].rearrange("p n t -> p (n t)").bitcast(F32).rearrange("p (a r u) -> p a r u", a=2, u=2)
            src = b[:].rearrange("p (a u r) -> p a r u", a=2, u=2)
            if eng == "S":
                nc.scalar.copy(out=dst, in_=src)
            else:
                nc.vector.tensor_copy(out=dst, in_=src)

        def quant(name, h):
            if name not in xq:
                xq[name] = keep.tile([128, 512], U32, name=f"{name}_q", align_bytes=64)
                xs[name] = keep.tile([128, 512], U8, name=f"{name}_s", align_bytes=64)
            cols = slice(256 * h, 256 * h + 256)
            nc.vector.quantize_mx(
                out=xq[name][:, cols].bitcast(FP8X4),
                scales=xs[name][:, cols],
                in_=xt[name, h][:].rearrange("p n t -> p (n t)"),
            )

        wp = {n: keep.tile([128, W], U32, name=f"{n}_p", align_bytes=64) for n in ("psi", "phi", "the")}
        ws = {n: keep.tile([128, W], U8, name=f"{n}_s", align_bytes=64) for n in ("psi", "phi", "the")}

        def order_scales(name):
            nc.vector.tensor_copy(
                out=ws[name][:].rearrange("p (g j m) -> p g m j", g=2, j=4),
                in_=s_raw[name][:].rearrange("p (g m j) -> p g m j", g=2, j=4),
            )

        def order_words(name, g):
            cols = slice(512 * g, 512 * g + 512)
            nc.vector.tensor_copy(
                out=wp[name][:, cols].bitcast(I32).rearrange("p (j m) -> p m j", j=4),
                in_=w_raw[name][:, cols].bitcast(I32).rearrange("p (m j) -> p m j", j=4),
            )

        def product(dst, name, g, j, x, cols):
            c0 = 512 * g + 128 * j
            nc.tensor.matmul_mx(
                out=dst,
                lhsT=wp[name][:, c0 : c0 + 128].bitcast(FP8X4),
                lhsT_scale=ws[name][:, c0 : c0 + 128],
                rhs=xq[x][:, cols].bitcast(FP8X4),
                rhs_scale=xs[x][:, cols],
                start=True,
                stop=True,
            )

        vs, vq, ti, tq, ts = {}, {}, {}, {}, {}
        halves = (slice(0, 256), slice(256, 512))

        def visible(c, g, h):
            if (c, g) not in vs:
                vs[c, g] = work.tile([128, 4, 512], F32, name="vs", bufs=3, align_bytes=64)
            for jp in (0, 2):
                b = bank("vis")
                for i in range(2):
                    product(b[:, 256 * i : 256 * i + 256], "psi", g, jp + i, f"v{c}", halves[h])
                nc.scalar.activation(
                    out=vs[c, g][:, jp : jp + 2, halves[h]], in_=b[:].rearrange("p (j n) -> p j n", j=2), func=SIGMOID
                )

        def weigh(c, g, jp, engs):
            if (c, g) not in vq:
                vq[c, g] = work.tile([128, 4, 512], F32, name="vq", bufs=3, align_bytes=64)
            for i in range(2):
                j = 2 * jp + i
                src, dst, scalar = vs[c, g][:, j, :], vq[c, g][:, j, :], q_sb[:, g, j : j + 1]
                if engs[i] == "V":
                    nc.vector.tensor_scalar(out=dst, in0=src, scalar1=scalar, scalar2=None, op0=MULT)
                else:
                    nc.gpsimd.tensor_scalar(out=dst, in0=src, scalar1=scalar, scalar2=0.0, op0=MULT, op1=ADD)

        def reflect(c, g, h):
            if h == 0:
                ti[c, g] = work.tile([128, 512, 4], BF16, name="ti", bufs=3, align_bytes=64)
            for k in (2 * h, 2 * h + 1):
                cols = slice(128 * k, 128 * k + 128)
                b = bank("ref")
                for j in range(4):
                    product(b[:, 128 * j : 128 * j + 128], "phi", g, j, f"r{c}", cols)
                nc.vector.tensor_tensor(
                    out=ti[c, g][:, cols, :].rearrange("p (c i) j -> p c j i", i=4),
                    in0=b[:].rearrange("p (j c i) -> p c j i", j=4, i=4),
                    in1=vq[c, g][:, :, cols].rearrange("p j (c i) -> p c j i", i=4),
                    op=MULT,
                )

        def quant_tr(c, g, cols):
            if (c, g) not in tq:
                tq[c, g] = keep.tile([128, 512], U32, name=f"tq{c}{g}", align_bytes=64)
                ts[c, g] = keep.tile([128, 512], U8, name=f"ts{c}{g}", align_bytes=64)
            nc.vector.quantize_mx(
                out=tq[c, g][:, cols].bitcast(FP8X4),
                scales=ts[c, g][:, cols],
                in_=ti[c, g][:, cols, :].rearrange("p n j -> p (n j)"),
            )

        rt = {g: keep.tile([128, N, 4], BF16, name=f"rt{g}", align_bytes=64) for g in range(2)}
        rq = {g: keep.tile([128, N], U32, name=f"rq{g}", align_bytes=64) for g in range(2)}
        rs = {g: keep.tile([128, N], U8, name=f"rs{g}", align_bytes=64) for g in range(2)}

        def radiance(g, h, engs="SS"):
            for k in (2 * h, 2 * h + 1):
                cols = slice(128 * k, 128 * k + 128)
                b = bank("fin")
                for j in range(4):
                    product(b[:, 128 * j : 128 * j + 128], "the", g, j, "l", cols)
                src = b[:].rearrange("p (j n) -> p n j", j=4)
                if engs[k % 2] == "S":
                    nc.scalar.copy(out=rt[g][:, cols, :], in_=src)
                else:
                    nc.vector.tensor_copy(out=rt[g][:, cols, :], in_=src)

        def quant_rad(g):
            nc.vector.quantize_mx(
                out=rq[g][:].bitcast(FP8X4), scales=rs[g][:], in_=rt[g][:].rearrange("p n j -> p (n j)")
            )

        res = {c: keep.tile([128, 4, N], F32, name=f"res{c}", align_bytes=64) for c in range(2)}
        ob = {c: keep.tile([128, N, 4], BF16, name=f"ob{c}", align_bytes=64) for c in range(2)}
        oq = {c: keep.tile([128, N], U32, name=f"oq{c}", align_bytes=64) for c in range(2)}
        osc = keep.tile([128, 2, N], U8, name="osc", align_bytes=64)

        def transport(b, c, t, g, start, stop):
            nc.tensor.matmul_mx(
                out=b[:],
                lhsT=tq[c, g][:, 128 * t : 128 * t + 128].bitcast(FP8X4),
                lhsT_scale=ts[c, g][:, 128 * t : 128 * t + 128],
                rhs=rq[g][:].bitcast(FP8X4),
                rhs_scale=rs[g][:],
                start=start,
                stop=stop,
            )

        def result(b, c, t, eng):
            if eng == "S":
                nc.scalar.activation(out=res[c][:, t, :], in_=b[:], func=COPY, scale=COEF)
            else:
                nc.vector.tensor_scalar(out=res[c][:, t, :], in0=b[:], scalar1=COEF, scalar2=None, op0=MULT)
            if t % 2 == 1:
                rows = out_0[512 * c : 512 * c + 512, :].rearrange("(p t) n -> p t n", t=4)
                nc.sync.dma_start(out=rows[:, t - 1 : t + 1, :], in_=res[c][:, t - 1 : t + 1, :])

        def final0(h, engs):
            for i in range(2):
                t = 2 * h + i
                b = bank("fin")
                transport(b, 0, t, 0, True, False)
                transport(b, 0, t, 1, False, True)
                result(b, 0, t, engs[i])

        tail = {}

        def open_final1():
            for t in range(4):
                tail[t] = bank("fin" if t < 2 else "tp")
                transport(tail[t], 1, t, 0, True, False)

        def close_final1(h, engs):
            for i in range(2):
                t = 2 * h + i
                transport(tail[t], 1, t, 1, False, True)
                result(tail[t], 1, t, engs[i])

        def regroup(c, h, eng):
            cols = slice(256 * h, 256 * h + 256)
            src = res[c][:, :, cols].rearrange("p t (d i) -> p d t i", i=4)
            dst = ob[c][:, cols, :].rearrange("p (d i) t -> p d t i", i=4)
            if eng == "S":
                nc.scalar.copy(out=dst, in_=src)
            else:
                nc.vector.tensor_copy(out=dst, in_=src)

        planes_done = {0: [], 1: []}

        def quant_out(c, h):
            cols = slice(256 * h, 256 * h + 256)
            nc.vector.quantize_mx(
                out=oq[c][:, cols].bitcast(FP8X4),
                scales=osc[:, c, cols],
                in_=ob[c][:, cols, :].rearrange("p n t -> p (n t)"),
            )
            planes_done[c].append(h)
            words = out_1[c].rearrange("p m t -> p (m t)")
            if c == 1:
                nc.sync.dma_start(
                    out=words[:, 1024 * h : 1024 * h + 1024].bitcast(I32), in_=oq[c][:, cols].bitcast(I32)
                )
            elif len(planes_done[c]) == 2:
                nc.sync.dma_start(out=words.bitcast(I32), in_=oq[c][:].bitcast(I32))

        def store_scales():
            for s in range(4):
                nc.sync.dma_start(
                    out=out_2[:, 4 * s : 4 * s + 4, :].rearrange("c s m -> s c m").bitcast(I32),
                    in_=osc[32 * s : 32 * s + 4, :, :].bitcast(I32),
                )

        order_words("psi", 0)
        order_scales("psi")
        turn("v0", 0, "S")
        quant("v0", 0)
        turn("v0", 1, "V")
        order_words("psi", 1)
        quant("v0", 1)
        visible(0, 0, 0)
        order_words("phi", 0)
        turn("r0", 0, "S")
        order_words("phi", 1)
        turn("r0", 1, "V")
        quant("r0", 0)
        visible(0, 0, 1)
        turn("l", 0, "V")
        quant("r0", 1)
        order_scales("phi")
        visible(0, 1, 0)
        order_words("the", 0)
        order_words("the", 1)
        turn("l", 1, "S")
        turn("v1", 0, "S")
        quant("v1", 0)
        quant("l", 1)
        weigh(0, 0, 0, "GG")
        quant("l", 0)
        order_scales("the")
        visible(0, 1, 1)
        weigh(0, 0, 1, "GG")
        reflect(0, 0, 0)
        turn("v1", 1, "S")
        visible(1, 0, 0)
        quant("v1", 1)
        radiance(0, 0, "SS")
        reflect(0, 0, 1)
        quant_tr(0, 0, halves[0])
        weigh(0, 1, 0, "GG")
        visible(1, 0, 1)
        quant_tr(0, 0, halves[1])
        turn("r1", 0, "V")
        turn("r1", 1, "V")
        radiance(1, 0, "SS")
        quant("r1", 0)
        quant("r1", 1)
        visible(1, 1, 0)
        weigh(0, 1, 1, "GG")
        reflect(0, 1, 0)
        weigh(1, 0, 0, "GG")
        weigh(1, 0, 1, "GG")
        radiance(0, 1, "SS")
        reflect(0, 1, 1)
        visible(1, 1, 1)
        quant_rad(0)
        radiance(1, 1, "SS")
        quant_tr(0, 1, halves[0])
        reflect(1, 0, 0)
        quant_rad(1)
        weigh(1, 1, 0, "GG")
        reflect(1, 0, 1)
        quant_tr(0, 1, halves[1])
        quant_tr(1, 0, halves[0])
        weigh(1, 1, 1, "GG")
        final0(0, "SS")
        reflect(1, 1, 0)
        quant_tr(1, 0, halves[1])
        quant_tr(1, 1, halves[0])
        final0(1, "SS")
        reflect(1, 1, 1)
        open_final1()
        regroup(0, 1, "S")
        quant_tr(1, 1, halves[1])
        regroup(0, 0, "V")
        close_final1(0, "SS")
        close_final1(1, "VS")
        quant_out(0, 1)
        regroup(1, 1, "V")
        quant_out(0, 0)
        regroup(1, 0, "S")
        quant_out(1, 1)
        quant_out(1, 0)
        store_scales()
